import numpy as np
import ml_dtypes


def mxq(x, axis, fmt="e4m3"):
    dtype, down = {"e4m3": (ml_dtypes.float8_e4m3fn, 7), "e5m2": (ml_dtypes.float8_e5m2, 14)}[fmt]
    v = np.moveaxis(np.asarray(x, np.float32).astype(ml_dtypes.bfloat16).astype(np.float64), axis, -1)
    blocks = v.reshape(v.shape[:-1] + (-1, 32))
    amax = np.abs(blocks).max(-1, keepdims=True)
    byte = np.maximum(np.where(amax > 0, np.frexp(amax)[1] - 1 + 127, 0) - down, 1)
    scale = np.exp2(byte - 127.0)
    codes = (blocks / scale).astype(np.float32).astype(dtype).astype(np.float64)
    return np.moveaxis((codes * scale).reshape(v.shape), -1, axis)


WIDE = False


def mx_kscale(k):
    if not WIDE:
        return np.ones(k)
    levels = np.array([10, -10, 5, -5, 0])
    if k % 512:
        return np.exp2(np.random.permutation(np.resize(levels, k // 32))).repeat(32)
    a = np.empty((k // 512, 16))
    for p in range(k // 512):
        a[p, :8] = np.random.permutation(np.resize(levels, 8))
        for g in range(8):
            far = levels[np.abs(levels - a[p, g]) >= 10]
            a[p, g + 8] = far[np.random.randint(len(far))]
    return np.exp2(a.ravel()).repeat(32)


def f64(x):
    return np.asarray(x).astype(np.float64)


def striped(idx):
    return np.tile(np.asarray(idx).reshape(-1, 16).T, (8, 1)).astype(np.uint16)


def unstriped(offs):
    return offs[:16].T.reshape(-1).astype(np.int64)


E2M1 = np.array([0.0, 0.5, 1.0, 1.5, 2.0, 3.0, 4.0, 6.0, -0.0, -0.5, -1.0, -1.5, -2.0, -3.0, -4.0, -6.0])


def pack_weight(w, fmt):
    k, n = w.shape
    w = f64(np.asarray(w, np.float32).astype(ml_dtypes.bfloat16)).reshape(k // 32, 32, n)
    amax = np.abs(w).max(1)
    if fmt == "e4m3":
        byte = np.frexp(amax)[1] - 1 + 127 - 7
    else:
        mant, ex = np.frexp(amax / 6.0)
        byte = np.where(mant > 0.5, ex, ex - 1) + 127
    byte = np.clip(np.where(amax > 0, byte, 1), 1, 254)
    scaled = (w * np.exp2(127.0 - byte)[:, None, :]).reshape(k, n).astype(np.float32)
    by_word = np.ascontiguousarray(scaled.reshape(k // 512, 128, 4, n).transpose(0, 1, 3, 2))
    if fmt == "e4m3":
        words = by_word.astype(ml_dtypes.float8_e4m3fn).view(np.uint8)
    else:
        c = by_word.astype(ml_dtypes.float4_e2m1fn).view(np.uint8) & 0xF
        words = (c[..., 0::2] | (c[..., 1::2] << 4)).reshape(k // 512, 128, 2 * n)
    return np.ascontiguousarray(words), np.ascontiguousarray(byte.astype(np.uint8).reshape(k // 512, 16, n))


def unpack_weight(words, scales, fmt):
    g, _, n = scales.shape
    words = np.ascontiguousarray(words).reshape(g, 128, n, -1)
    if fmt == "e4m3":
        vals = words.view(ml_dtypes.float8_e4m3fn).astype(np.float64)
    else:
        nib = np.empty((g, 128, n, 4), np.uint8)
        nib[..., 0::2] = words & 0xF
        nib[..., 1::2] = words >> 4
        vals = E2M1[nib]
    vals = vals * np.repeat(np.exp2(scales.astype(np.float64) - 127.0), 8, axis=1)[..., None]
    return vals.transpose(0, 1, 3, 2).reshape(g * 512, n)


def bf(x):
    return np.asarray(x, np.float32).astype(ml_dtypes.bfloat16)


def planes(Y):
    r, m = Y.shape
    b = f64(bf(Y)).reshape(r // 32, 32, m)
    amax = np.abs(b).max(1)
    byte = np.clip(np.where(amax > 0, np.frexp(amax)[1] - 1 + 127 - 7, 1), 1, 254)
    codes = (b * np.exp2(127.0 - byte)[:, None, :]).reshape(r, m).astype(np.float32).astype(ml_dtypes.float8_e4m3fn).view(np.uint8)
    words = codes.reshape(r // 512, 128, 4, m).transpose(0, 1, 3, 2)
    return np.ascontiguousarray(words), np.ascontiguousarray(byte.astype(np.uint8).reshape(r // 512, 16, m))


D, T, I, Q, E, U, V = 512, 2048, 512, 256, 512, 512, 512


def setup_inputs():
    n = np.random.standard_normal
    idx = np.random.permutation(T)[:I]
    idx2 = np.random.randint(0, U, I)
    idx3 = np.random.randint(0, V, I)
    fd = mx_kscale(D)
    fi = mx_kscale(I)
    ti = np.ones(T)
    ti[idx] = fi
    keysp = pack_weight(n((D, T)) / fd[:, None], "e2m1")
    return {
        "query": (n((D, Q)) * 0.25 / np.sqrt(D) * fd[:, None]).astype(np.float32),
        "keys_words": keysp[0],
        "keys_scales": keysp[1],
        "bh": (0.25 * n((Q, U))).astype(np.float32),
        "bw": (0.25 * n((Q, V))).astype(np.float32),
        "size": (np.random.uniform(0.5, 2.0, (1, I)) * fi).astype(np.float32),
        "vals": (n((E, T)) / ti).astype(np.float32),
        "offs": striped(idx),
        "offs2": striped(idx2),
        "offs3": striped(idx3),
    }


def reference(query, keys_words, keys_scales, bh, bw, size, vals, offs, offs2, offs3):
    idx = unstriped(offs)
    idx2 = unstriped(offs2)
    idx3 = unstriped(offs3)
    keysu = unpack_weight(keys_words, keys_scales, "e2m1")
    queryq = mxq(f64(query), 0, "e4m3")
    keysidxg = keysu[:, idx]
    a = queryq.T @ keysidxg
    s = a + f64(bh)[:, idx2] + f64(bw)[:, idx3]
    p = np.exp(s - np.max(s, axis=1, keepdims=True))
    w = p * f64(size) / np.sum(p, axis=1, keepdims=True)
    wt = w.T
    vt = f64(vals)[:, idx].T
    vtq = mxq(vt, 0, "e4m3")
    wtq = mxq(wt, 0, "e4m3")
    o = vtq.T @ wtq
    words, scales = planes(o)
    return o, words, scales

@@ -1,0 +1,194 @@
+from contextlib import ExitStack
+
+import concourse.mybir as mybir
+from concourse.masks import make_identity
+
+F32 = mybir.dt.float32
+BF16 = mybir.dt.bfloat16
+I32 = mybir.dt.int32
+U32 = mybir.dt.uint32
+U16 = mybir.dt.uint16
+U8 = mybir.dt.uint8
+FP8X4 = mybir.dt.float8_e4m3fn_x4
+FP4X4 = mybir.dt.float4_e2m1fn_x4
+ALU = mybir.AluOpType
+ACT = mybir.ActivationFunctionType
+AX = mybir.AxisListType
+
+P = 128
+PACK = 4
+D, T, I, Q, E, U = 512, 2048, 512, 256, 512, 512
+FLOPS = 2 * D * Q * I + 2 * I * E * Q
+COPY_WINDOW = 704
+ADD_WINDOW = 528
+
+
+def tile_attend_decomposedbias_pl_kernel(tc, query, keys_words, keys_scales, bh, bw, size, vals,
+                                          offs, offs2, offs3, out_0, out_1, out_2):
+    nc = tc.nc
+    with ExitStack() as ctx:
+        keep = ctx.enter_context(tc.tile_pool(name="keep", bufs=1))
+        psum = ctx.enter_context(tc.psum_pool(name="psum", bufs=1))
+
+        def sb(shape, dtype, name):
+            return keep.tile(shape, dtype, name=name, align_bytes=64)
+
+        tok_list = sb([P, I // 16], U16, "tok_list")
+        h_list = sb([P, I // 16], U16, "h_list")
+        w_list = sb([P, I // 16], U16, "w_list")
+        key_words = sb([P, T], U16, "key_words")
+        key_bytes = sb([P, T], U8, "key_bytes")
+        q_raw = sb([P, PACK, Q], F32, "q_raw")
+        bh_win = [sb([P, COPY_WINDOW], F32, "bh_win0"), sb([P, ADD_WINDOW], F32, "bh_win1")]
+        bw_win = [sb([P, ADD_WINDOW], F32, "bw_win%d" % h) for h in range(2)]
+        val_win = [sb([P, T], F32, "val_win%d" % r) for r in range(PACK)]
+        size_col = sb([P, PACK], F32, "size_col")
+        ident = sb([P, P], F32, "ident")
+        warm = sb([P, 1], F32, "warm")
+        warm_out = sb([P, 1], F32, "warm_out")
+
+        nc.vector.memset(key_bytes[:].bitcast(I32), 0)
+        for win in bh_win + bw_win:
+            nc.vector.memset(win[:, U:], 0.0)
+        nc.vector.memset(warm[:], 0.0)
+        nc.scalar.activation(warm_out[:], warm[:], ACT.Exp)
+
+        val_rows = vals.rearrange("(p r) t -> r p t", r=PACK)
+        nc.sync.dma_start(h_list[:], offs2)
+        nc.sync.dma_start(bh_win[0][:, :U], bh[0:P, :])
+        nc.sync.dma_start(w_list[:], offs3)
+        nc.sync.dma_start(bw_win[0][:, :U], bw[0:P, :])
+        nc.sync.dma_start(tok_list[:], offs)
+        nc.sync.dma_start(key_words[:].bitcast(I32), keys_words[0].bitcast(I32))
+        nc.sync.dma_start(q_raw[:], query.rearrange("(p j) q -> p j q", j=PACK))
+        for g in range(4):
+            nc.sync.dma_start(key_bytes[32 * g:32 * g + 4, :].bitcast(I32),
+                              keys_scales[0, 4 * g:4 * g + 4, :].bitcast(I32))
+        nc.sync.dma_start(val_win[0][:], val_rows[0])
+        nc.sync.dma_start(bh_win[1][:, :U], bh[P:2 * P, :])
+        nc.sync.dma_start(bw_win[1][:, :U], bw[P:2 * P, :])
+        for r in range(1, PACK):
+            nc.sync.dma_start(val_win[r][:], val_rows[r])
+        nc.gpsimd.dma_start(size_col[:], size.rearrange("o (s t) -> s (o t)", t=PACK))
+        make_identity(nc, ident[:])
+
+        size_ps = psum.tile([P, PACK, P], F32, name="size_ps")
+        for t in range(PACK):
+            nc.tensor.transpose(size_ps[:, t, :], size_col[:, t:t + 1].to_broadcast([P, P]), ident[:])
+
+        bias0a = sb([P, I], F32, "bias0a")
+        bias0 = sb([P, I], F32, "bias0")
+        nc.vector.tensor_copy(bias0a[:], bh_win[0][:].indirect(h_list[:]))
+        nc.vector.tensor_tensor(bias0[:], bw_win[0][:].indirect(w_list[:]), bias0a[:], ALU.add)
+
+        k_words = sb([P, I], U16, "k_words")
+        k_bytes = sb([P, I], U8, "k_bytes")
+        nc.vector.tensor_copy(k_words[:], key_words[:].indirect(tok_list[:]))
+        nc.vector.tensor_copy(k_bytes[:], key_bytes[:].indirect(tok_list[:]))
+
+        q_grp = sb([P, Q, PACK], BF16, "q_grp")
+        nc.scalar.copy(q_grp[:].rearrange("p (c i) t -> p c t i", i=4),
+                       q_raw[:].rearrange("p t (c i) -> p c t i", i=4))
+        q_codes = sb([P, Q], U32, "q_codes")
+        q_scales = sb([P, Q], U8, "q_scales")
+        nc.vector.quantize_mx(out=q_codes[:].bitcast(FP8X4), scales=q_scales[:],
+                              in_=q_grp[:].rearrange("p q t -> p (q t)"))
+
+        score_ps = []
+        for h in range(2):
+            bank = psum.tile([P, I], F32, name="score_ps%d" % h, tag="row%d" % h)
+            cols = slice(h * P, (h + 1) * P)
+            nc.tensor.matmul_mx(out=bank[:], lhsT=q_codes[:, cols].bitcast(FP8X4), lhsT_scale=q_scales[:, cols],
+                                rhs=k_words[:].bitcast(FP4X4), rhs_scale=k_bytes[:], start=True, stop=True)
+            score_ps.append(bank)
+
+        v_codes = [sb([P, P], U32, "v_codes%d" % r) for r in range(PACK)]
+        v_scales = [sb([P, P], U8, "v_scales%d" % r) for r in range(PACK)]
+        v_grp = [sb([P, P, PACK], BF16, "v_grp%d" % r) for r in range(PACK)]
+        w_grp = [sb([P, P, PACK], BF16, "w_grp%d" % h) for h in range(2)]
+        w_codes = sb([P, Q], U32, "w_codes")
+        w_scales = sb([P, Q], U8, "w_scales")
+
+        def turn(src, dst, bank):
+            words = src[:].bitcast(F32)
+            for u in range(2):
+                nc.tensor.transpose(bank[:, u, :], words[:, u:I // 2:2], ident[:])
+            nc.scalar.copy(dst[:].rearrange("p c t -> p (c t)").bitcast(F32).rearrange("p (c u) -> p c u", u=2),
+                           bank[:].rearrange("p u c -> p c u"))
+
+        def gather_vals(r):
+            picked = sb([P, I], BF16, "v_picked%d" % r)
+            nc.vector.tensor_copy(picked[:], val_win[r][:].indirect(tok_list[:]))
+            bank = psum.tile([P, 2, P], F32, name="v_ps%d" % r, tag="v_ps", bufs=2)
+            turn(picked, v_grp[r], bank)
+
+        def quant_vals(r):
+            nc.vector.quantize_mx(out=v_codes[r][:].bitcast(FP8X4), scales=v_scales[r][:],
+                                  in_=v_grp[r][:].rearrange("p c t -> p (c t)"))
+
+        s = [sb([P, I], F32, "s%d" % h) for h in range(2)]
+        p = [sb([P, I], F32, "p%d" % h) for h in range(2)]
+        neg_max = [sb([P, 1], F32, "neg_max%d" % h) for h in range(2)]
+        row_sum = [sb([P, 1], F32, "row_sum%d" % h) for h in range(2)]
+        inv_sum = [sb([P, 1], F32, "inv_sum%d" % h) for h in range(2)]
+
+        def softmax_head(h):
+            nc.vector.tensor_reduce(neg_max[h][:], s[h][:], AX.X, ALU.max, negate=True)
+            nc.scalar.activation(p[h][:], s[h][:], ACT.Exp, bias=neg_max[h][:], accum_out=row_sum[h][:])
+
+        def weights(h):
+            nc.vector.reciprocal(inv_sum[h][:], row_sum[h][:])
+            w = sb([P, I], BF16, "w%d" % h)
+            nc.vector.scalar_tensor_tensor(w[:].rearrange("p (s t) -> p s t", t=PACK),
+                                           p[h][:].rearrange("p (s t) -> p s t", t=PACK), inv_sum[h][:],
+                                           size_ps[:].rearrange("p t s -> p s t"), ALU.mult, ALU.mult)
+            bank = psum.tile([P, 2, P], F32, name="w_ps%d" % h, tag="row%d" % h)
+            turn(w, w_grp[h], bank)
+
+        def quant_weights(h):
+            cols = slice(h * P, (h + 1) * P)
+            nc.vector.quantize_mx(out=w_codes[:, cols].bitcast(FP8X4), scales=w_scales[:, cols],
+                                  in_=w_grp[h][:].rearrange("p c t -> p (c t)"))
+
+        a1 = sb([P, I], F32, "a1")
+        t1 = sb([P, I], F32, "t1")
+        nc.scalar.copy(a1[:], score_ps[1][:])
+
+        gather_vals(0)
+        nc.vector.tensor_tensor(s[0][:], score_ps[0][:], bias0[:], ALU.add)
+        softmax_head(0)
+        nc.vector.tensor_tensor(t1[:], bh_win[1][:].indirect(h_list[:]), a1[:], ALU.add)
+        nc.vector.tensor_tensor(s[1][:], bw_win[1][:].indirect(w_list[:]), t1[:], ALU.add)
+        softmax_head(1)
+        weights(0)
+        quant_vals(0)
+        gather_vals(1)
+        weights(1)
+        quant_weights(0)
+        gather_vals(2)
+        quant_vals(1)
+        quant_weights(1)
+        gather_vals(3)
+        quant_vals(2)
+        quant_vals(3)
+
+        y = sb([P, PACK, Q], F32, "y")
+        out_rows = out_0.rearrange("(p r) q -> r p q", r=PACK)
+        for r in range(PACK):
+            bank = psum.tile([P, Q], F32, name="o_ps%d" % r, tag="o_ps", bufs=2)
+            nc.tensor.matmul_mx(out=bank[:], lhsT=v_codes[r][:].bitcast(FP8X4), lhsT_scale=v_scales[r][:],
+                                rhs=w_codes[:].bitcast(FP8X4), rhs_scale=w_scales[:], start=True, stop=True)
+            nc.scalar.copy(y[:, r, :], bank[:])
+            nc.sync.dma_start(out_rows[r], y[:, r, :])
+
+        y_grp = sb([P, Q, PACK], BF16, "y_grp")
+        nc.vector.tensor_copy(y_grp[:].rearrange("p (c i) t -> p c t i", i=4),
+                              y[:].rearrange("p t (c i) -> p c t i", i=4))
+        y_codes = sb([P, Q], U32, "y_codes")
+        y_scales = sb([P, Q], U8, "y_scales")
+        nc.vector.quantize_mx(out=y_codes[:].bitcast(FP8X4), scales=y_scales[:],
+                              in_=y_grp[:].rearrange("p q t -> p (q t)"))
+        nc.sync.dma_start(out_1[0].rearrange("p c r -> p (c r)").bitcast(I32), y_codes[:].bitcast(I32))
+        for g in range(4):
+            queue = nc.scalar if g % 2 else nc.sync
+            queue.dma_start(out_2[0, 4 * g:4 * g + 4, :].bitcast(I32), y_scales[32 * g:32 * g + 4, :].bitcast(I32))

@@ -19,7 +19,6 @@ P = 128
 PACK = 4
 D, T, I, Q, E, U = 512, 2048, 512, 256, 512, 512
 FLOPS = 2 * D * Q * I + 2 * I * E * Q
-COPY_WINDOW = 704
 ADD_WINDOW = 528
 
 
@@ -30,8 +29,8 @@ def tile_attend_decomposedbias_pl_kernel(tc, query, keys_words, keys_scales, bh,
         keep = ctx.enter_context(tc.tile_pool(name="keep", bufs=1))
         psum = ctx.enter_context(tc.psum_pool(name="psum", bufs=1))
 
-        def sb(shape, dtype, name):
-            return keep.tile(shape, dtype, name=name, align_bytes=64)
+        def sb(shape, dtype, name, after=None):
+            return keep.tile(shape, dtype, name=name, tag=after or name, align_bytes=64)
 
         tok_list = sb([P, I // 16], U16, "tok_list")
         h_list = sb([P, I // 16], U16, "h_list")
@@ -39,9 +38,10 @@ def tile_attend_decomposedbias_pl_kernel(tc, query, keys_words, keys_scales, bh,
         key_words = sb([P, T], U16, "key_words")
         key_bytes = sb([P, T], U8, "key_bytes")
         q_raw = sb([P, PACK, Q], F32, "q_raw")
-        bh_win = [sb([P, COPY_WINDOW], F32, "bh_win0"), sb([P, ADD_WINDOW], F32, "bh_win1")]
+        bh_win = [sb([P, ADD_WINDOW], F32, "bh_win%d" % h) for h in range(2)]
         bw_win = [sb([P, ADD_WINDOW], F32, "bw_win%d" % h) for h in range(2)]
-        val_win = [sb([P, T], F32, "val_win%d" % r) for r in range(PACK)]
+        val_win = [None] + [sb([P, T], F32, "val_win%d" % r) for r in range(1, PACK)]
+        val_part = [sb([P, T // 2], F32, "val_part%d" % j) for j in range(2)]
         size_col = sb([P, PACK], F32, "size_col")
         ident = sb([P, P], F32, "ident")
         warm = sb([P, 1], F32, "warm")
@@ -54,20 +54,21 @@ def tile_attend_decomposedbias_pl_kernel(tc, query, keys_words, keys_scales, bh,
         nc.scalar.activation(warm_out[:], warm[:], ACT.Exp)
 
         val_rows = vals.rearrange("(p r) t -> r p t", r=PACK)
-        nc.sync.dma_start(h_list[:], offs2)
-        nc.sync.dma_start(bh_win[0][:, :U], bh[0:P, :])
-        nc.sync.dma_start(w_list[:], offs3)
-        nc.sync.dma_start(bw_win[0][:, :U], bw[0:P, :])
         nc.sync.dma_start(tok_list[:], offs)
         nc.sync.dma_start(key_words[:].bitcast(I32), keys_words[0].bitcast(I32))
-        nc.sync.dma_start(q_raw[:], query.rearrange("(p j) q -> p j q", j=PACK))
+        nc.sync.dma_start(h_list[:], offs2)
+        nc.sync.dma_start(w_list[:], offs3)
         for g in range(4):
-            nc.sync.dma_start(key_bytes[32 * g:32 * g + 4, :].bitcast(I32),
-                              keys_scales[0, 4 * g:4 * g + 4, :].bitcast(I32))
-        nc.sync.dma_start(val_win[0][:], val_rows[0])
-        nc.sync.dma_start(bh_win[1][:, :U], bh[P:2 * P, :])
-        nc.sync.dma_start(bw_win[1][:, :U], bw[P:2 * P, :])
-        for r in range(1, PACK):
+            nc.scalar.dma_start(key_bytes[32 * g:32 * g + 4, :].bitcast(I32),
+                                keys_scales[0, 4 * g:4 * g + 4, :].bitcast(I32))
+        nc.sync.dma_start(q_raw[:], query.rearrange("(p j) q -> p j q", j=PACK))
+        nc.sync.dma_start(val_win[1][:], val_rows[1])
+        for win, table in ((bh_win, bh), (bw_win, bw)):
+            for h in range(2):
+                nc.sync.dma_start(win[h][:, :U], table[h * P:(h + 1) * P, :])
+        for j in range(2):
+            nc.sync.dma_start(val_part[j][:], val_rows[0][:, j * T // 2:(j + 1) * T // 2])
+        for r in range(2, PACK):
             nc.sync.dma_start(val_win[r][:], val_rows[r])
         nc.gpsimd.dma_start(size_col[:], size.rearrange("o (s t) -> s (o t)", t=PACK))
         make_identity(nc, ident[:])
@@ -75,11 +76,6 @@ def tile_attend_decomposedbias_pl_kernel(tc, query, keys_words, keys_scales, bh,
         size_ps = psum.tile([P, PACK, P], F32, name="size_ps")
         for t in range(PACK):
             nc.tensor.transpose(size_ps[:, t, :], size_col[:, t:t + 1].to_broadcast([P, P]), ident[:])
-
-        bias0a = sb([P, I], F32, "bias0a")
-        bias0 = sb([P, I], F32, "bias0")
-        nc.vector.tensor_copy(bias0a[:], bh_win[0][:].indirect(h_list[:]))
-        nc.vector.tensor_tensor(bias0[:], bw_win[0][:].indirect(w_list[:]), bias0a[:], ALU.add)
 
         k_words = sb([P, I], U16, "k_words")
         k_bytes = sb([P, I], U8, "k_bytes")
@@ -102,83 +98,88 @@ def tile_attend_decomposedbias_pl_kernel(tc, query, keys_words, keys_scales, bh,
                                 rhs=k_words[:].bitcast(FP4X4), rhs_scale=k_bytes[:], start=True, stop=True)
             score_ps.append(bank)
 
-        v_codes = [sb([P, P], U32, "v_codes%d" % r) for r in range(PACK)]
-        v_scales = [sb([P, P], U8, "v_scales%d" % r) for r in range(PACK)]
-        v_grp = [sb([P, P, PACK], BF16, "v_grp%d" % r) for r in range(PACK)]
-        w_grp = [sb([P, P, PACK], BF16, "w_grp%d" % h) for h in range(2)]
-        w_codes = sb([P, Q], U32, "w_codes")
-        w_scales = sb([P, Q], U8, "w_scales")
+        grp_a = sb([P, 4, P, PACK], BF16, "grp_a")
+        grp_v = [sb([P, P, PACK], BF16, "grp_v%d" % r) for r in (2, 3)]
+        v_dst = [grp_a[:, 2], grp_a[:, 3], grp_v[0][:], grp_v[1][:]]
 
         def turn(src, dst, bank):
             words = src[:].bitcast(F32)
             for u in range(2):
                 nc.tensor.transpose(bank[:, u, :], words[:, u:I // 2:2], ident[:])
-            nc.scalar.copy(dst[:].rearrange("p c t -> p (c t)").bitcast(F32).rearrange("p (c u) -> p c u", u=2),
+            nc.scalar.copy(dst.rearrange("p c t -> p (c t)").bitcast(F32).rearrange("p (c u) -> p c u", u=2),
                            bank[:].rearrange("p u c -> p c u"))
 
         def gather_vals(r):
             picked = sb([P, I], BF16, "v_picked%d" % r)
-            nc.vector.tensor_copy(picked[:], val_win[r][:].indirect(tok_list[:]))
+            if r == 0:
+                nc.scalar.activation(picked[:], val_half[:].indirect(tok_list[:]), ACT.Copy)
+            else:
+                nc.vector.tensor_copy(picked[:], val_win[r][:].indirect(tok_list[:]))
             bank = psum.tile([P, 2, P], F32, name="v_ps%d" % r, tag="v_ps", bufs=2)
-            turn(picked, v_grp[r], bank)
+            turn(picked, v_dst[r], bank)
 
-        def quant_vals(r):
-            nc.vector.quantize_mx(out=v_codes[r][:].bitcast(FP8X4), scales=v_scales[r][:],
-                                  in_=v_grp[r][:].rearrange("p c t -> p (c t)"))
-
-        s = [sb([P, I], F32, "s%d" % h) for h in range(2)]
-        p = [sb([P, I], F32, "p%d" % h) for h in range(2)]
         neg_max = [sb([P, 1], F32, "neg_max%d" % h) for h in range(2)]
-        row_sum = [sb([P, 1], F32, "row_sum%d" % h) for h in range(2)]
-        inv_sum = [sb([P, 1], F32, "inv_sum%d" % h) for h in range(2)]
+        row_sum = sb([P, 2], F32, "row_sum")
 
         def softmax_head(h):
             nc.vector.tensor_reduce(neg_max[h][:], s[h][:], AX.X, ALU.max, negate=True)
-            nc.scalar.activation(p[h][:], s[h][:], ACT.Exp, bias=neg_max[h][:], accum_out=row_sum[h][:])
+            nc.scalar.activation(p[h][:], s[h][:], ACT.Exp, bias=neg_max[h][:], accum_out=row_sum[:, h:h + 1])
 
         def weights(h):
-            nc.vector.reciprocal(inv_sum[h][:], row_sum[h][:])
             w = sb([P, I], BF16, "w%d" % h)
             nc.vector.scalar_tensor_tensor(w[:].rearrange("p (s t) -> p s t", t=PACK),
-                                           p[h][:].rearrange("p (s t) -> p s t", t=PACK), inv_sum[h][:],
+                                           p[h][:].rearrange("p (s t) -> p s t", t=PACK), inv_sum[:, h:h + 1],
                                            size_ps[:].rearrange("p t s -> p s t"), ALU.mult, ALU.mult)
             bank = psum.tile([P, 2, P], F32, name="w_ps%d" % h, tag="row%d" % h)
-            turn(w, w_grp[h], bank)
+            turn(w, grp_a[:, h], bank)
 
-        def quant_weights(h):
-            cols = slice(h * P, (h + 1) * P)
-            nc.vector.quantize_mx(out=w_codes[:, cols].bitcast(FP8X4), scales=w_scales[:, cols],
-                                  in_=w_grp[h][:].rearrange("p c t -> p (c t)"))
-
-        a1 = sb([P, I], F32, "a1")
-        t1 = sb([P, I], F32, "t1")
-        nc.scalar.copy(a1[:], score_ps[1][:])
-
-        gather_vals(0)
-        nc.vector.tensor_tensor(s[0][:], score_ps[0][:], bias0[:], ALU.add)
-        softmax_head(0)
-        nc.vector.tensor_tensor(t1[:], bh_win[1][:].indirect(h_list[:]), a1[:], ALU.add)
-        nc.vector.tensor_tensor(s[1][:], bw_win[1][:].indirect(w_list[:]), t1[:], ALU.add)
-        softmax_head(1)
-        weights(0)
-        quant_vals(0)
+        score = [sb([P, I], F32, "score%d" % h) for h in range(2)]
+        part = [sb([P, I], F32, "part%d" % h) for h in range(2)]
+        s = [sb([P, I], F32, "s%d" % h) for h in range(2)]
+        for h in range(2):
+            nc.scalar.copy(score[h][:], score_ps[h][:])
         gather_vals(1)
-        weights(1)
-        quant_weights(0)
+        for h in range(2):
+            nc.vector.tensor_tensor(part[h][:], bh_win[h][:].indirect(h_list[:]), score[h][:], ALU.add)
+        for h in range(2):
+            nc.vector.tensor_tensor(s[h][:], bw_win[h][:].indirect(w_list[:]), part[h][:], ALU.add)
+        val_half = sb([P, T], BF16, "val_half")
+        for j in range(2):
+            nc.scalar.activation(val_half[:, j * T // 2:(j + 1) * T // 2], val_part[j][:], ACT.Copy)
+        gather_vals(0)
+        p = [sb([P, I], F32, "p0", after="val_half"), sb([P, I], F32, "p1", after="val_part1")]
+        softmax_head(0)
+        softmax_head(1)
         gather_vals(2)
-        quant_vals(1)
-        quant_weights(1)
+        inv_sum = sb([P, 2], F32, "inv_sum", after="val_win2")
+        nc.vector.reciprocal(inv_sum[:], row_sum[:])
+        weights(0)
+        weights(1)
         gather_vals(3)
-        quant_vals(2)
-        quant_vals(3)
+        a_codes = sb([P, 4 * P], U32, "a_codes", after="val_win3")
+        a_scales = sb([P, 4 * P], U8, "a_scales")
+        nc.vector.quantize_mx(out=a_codes[:].bitcast(FP8X4), scales=a_scales[:],
+                              in_=grp_a[:].rearrange("p a c t -> p (a c t)"))
+        v_codes = [a_codes[:, 2 * P:3 * P], a_codes[:, 3 * P:4 * P]]
+        v_scales = [a_scales[:, 2 * P:3 * P], a_scales[:, 3 * P:4 * P]]
+        for j in range(2):
+            codes = sb([P, P], U32, "b_codes%d" % j)
+            scales = sb([P, P], U8, "b_scales%d" % j)
+            nc.vector.quantize_mx(out=codes[:].bitcast(FP8X4), scales=scales[:],
+                                  in_=grp_v[j][:].rearrange("p c t -> p (c t)"))
+            v_codes.append(codes[:])
+            v_scales.append(scales[:])
 
         y = sb([P, PACK, Q], F32, "y")
         out_rows = out_0.rearrange("(p r) q -> r p q", r=PACK)
-        for r in range(PACK):
-            bank = psum.tile([P, Q], F32, name="o_ps%d" % r, tag="o_ps", bufs=2)
-            nc.tensor.matmul_mx(out=bank[:], lhsT=v_codes[r][:].bitcast(FP8X4), lhsT_scale=v_scales[r][:],
-                                rhs=w_codes[:].bitcast(FP8X4), rhs_scale=w_scales[:], start=True, stop=True)
-            nc.scalar.copy(y[:, r, :], bank[:])
+        for r, tag in enumerate(("row0", "row1", "o_ps2", "o_ps3")):
+            bank = psum.tile([P, Q], F32, name="o_ps%d" % r, tag=tag)
+            nc.tensor.matmul_mx(out=bank[:], lhsT=v_codes[r].bitcast(FP8X4), lhsT_scale=v_scales[r],
+                                rhs=a_codes[:, :Q].bitcast(FP8X4), rhs_scale=a_scales[:, :Q], start=True, stop=True)
+            if r == 1:
+                nc.vector.tensor_copy(y[:, r, :], bank[:])
+            else:
+                nc.scalar.copy(y[:, r, :], bank[:])
             nc.sync.dma_start(out_rows[r], y[:, r, :])
 
         y_grp = sb([P, Q, PACK], BF16, "y_grp")

@@ -19,6 +19,7 @@ P = 128
 PACK = 4
 D, T, I, Q, E, U = 512, 2048, 512, 256, 512, 512
 FLOPS = 2 * D * Q * I + 2 * I * E * Q
+COPY_WINDOW = 704
 ADD_WINDOW = 528
 
 
@@ -38,36 +39,36 @@ def tile_attend_decomposedbias_pl_kernel(tc, query, keys_words, keys_scales, bh,
         key_words = sb([P, T], U16, "key_words")
         key_bytes = sb([P, T], U8, "key_bytes")
         q_raw = sb([P, PACK, Q], F32, "q_raw")
-        bh_win = [sb([P, ADD_WINDOW], F32, "bh_win%d" % h) for h in range(2)]
+        bh_win = [sb([P, COPY_WINDOW], F32, "bh_win0"), sb([P, ADD_WINDOW], F32, "bh_win1")]
         bw_win = [sb([P, ADD_WINDOW], F32, "bw_win%d" % h) for h in range(2)]
-        val_win = [None] + [sb([P, T], F32, "val_win%d" % r) for r in range(1, PACK)]
-        val_part = [sb([P, T // 2], F32, "val_part%d" % j) for j in range(2)]
+        val_win = [sb([P, T], F32, "val_win%d" % r) for r in range(PACK)]
         size_col = sb([P, PACK], F32, "size_col")
         ident = sb([P, P], F32, "ident")
         warm = sb([P, 1], F32, "warm")
         warm_out = sb([P, 1], F32, "warm_out")
 
-        nc.vector.memset(key_bytes[:].bitcast(I32), 0)
+        nc.vector.memset(key_bytes[:, :T // 2].bitcast(I32), 0)
+        nc.gpsimd.memset(key_bytes[:, T // 2:].bitcast(I32), 0)
         for win in bh_win + bw_win:
             nc.vector.memset(win[:, U:], 0.0)
         nc.vector.memset(warm[:], 0.0)
         nc.scalar.activation(warm_out[:], warm[:], ACT.Exp)
 
         val_rows = vals.rearrange("(p r) t -> r p t", r=PACK)
+        nc.sync.dma_start(h_list[:], offs2)
+        nc.sync.dma_start(bh_win[0][:, :U], bh[0:P, :])
         nc.sync.dma_start(tok_list[:], offs)
         nc.sync.dma_start(key_words[:].bitcast(I32), keys_words[0].bitcast(I32))
-        nc.sync.dma_start(h_list[:], offs2)
         nc.sync.dma_start(w_list[:], offs3)
-        for g in range(4):
-            nc.scalar.dma_start(key_bytes[32 * g:32 * g + 4, :].bitcast(I32),
-                                keys_scales[0, 4 * g:4 * g + 4, :].bitcast(I32))
+        nc.sync.dma_start(bw_win[0][:, :U], bw[0:P, :])
         nc.sync.dma_start(q_raw[:], query.rearrange("(p j) q -> p j q", j=PACK))
+        for g in range(4):
+            nc.sync.dma_start(key_bytes[32 * g:32 * g + 4, :].bitcast(I32),
+                              keys_scales[0, 4 * g:4 * g + 4, :].bitcast(I32))
         nc.sync.dma_start(val_win[1][:], val_rows[1])
-        for win, table in ((bh_win, bh), (bw_win, bw)):
-            for h in range(2):
-                nc.sync.dma_start(win[h][:, :U], table[h * P:(h + 1) * P, :])
-        for j in range(2):
-            nc.sync.dma_start(val_part[j][:], val_rows[0][:, j * T // 2:(j + 1) * T // 2])
+        nc.sync.dma_start(bh_win[1][:, :U], bh[P:2 * P, :])
+        nc.sync.dma_start(val_win[0][:], val_rows[0])
+        nc.sync.dma_start(bw_win[1][:, :U], bw[P:2 * P, :])
         for r in range(2, PACK):
             nc.sync.dma_start(val_win[r][:], val_rows[r])
         nc.gpsimd.dma_start(size_col[:], size.rearrange("o (s t) -> s (o t)", t=PACK))
@@ -77,9 +78,13 @@ def tile_attend_decomposedbias_pl_kernel(tc, query, keys_words, keys_scales, bh,
         for t in range(PACK):
             nc.tensor.transpose(size_ps[:, t, :], size_col[:, t:t + 1].to_broadcast([P, P]), ident[:])
 
+        part = [sb([P, I], F32, "part%d" % h) for h in range(2)]
+        bias0 = sb([P, I], F32, "bias0")
+        nc.vector.tensor_copy(part[0][:], bh_win[0][:].indirect(h_list[:]))
         k_words = sb([P, I], U16, "k_words")
         k_bytes = sb([P, I], U8, "k_bytes")
         nc.vector.tensor_copy(k_words[:], key_words[:].indirect(tok_list[:]))
+        nc.vector.tensor_tensor(bias0[:], bw_win[0][:].indirect(w_list[:]), part[0][:], ALU.add)
         nc.vector.tensor_copy(k_bytes[:], key_bytes[:].indirect(tok_list[:]))
 
         q_grp = sb([P, Q, PACK], BF16, "q_grp")
@@ -133,22 +138,19 @@ def tile_attend_decomposedbias_pl_kernel(tc, query, keys_words, keys_scales, bh,
             bank = psum.tile([P, 2, P], F32, name="w_ps%d" % h, tag="row%d" % h)
             turn(w, grp_a[:, h], bank)
 
-        score = [sb([P, I], F32, "score%d" % h) for h in range(2)]
-        part = [sb([P, I], F32, "part%d" % h) for h in range(2)]
-        s = [sb([P, I], F32, "s%d" % h) for h in range(2)]
-        for h in range(2):
-            nc.scalar.copy(score[h][:], score_ps[h][:])
+        score1 = sb([P, I], F32, "score1")
+        nc.scalar.copy(score1[:], score_ps[1][:])
         gather_vals(1)
-        for h in range(2):
-            nc.vector.tensor_tensor(part[h][:], bh_win[h][:].indirect(h_list[:]), score[h][:], ALU.add)
-        for h in range(2):
-            nc.vector.tensor_tensor(s[h][:], bw_win[h][:].indirect(w_list[:]), part[h][:], ALU.add)
+        s = [sb([P, I], F32, "s0", after="val_win1"), sb([P, I], F32, "s1")]
+        nc.vector.tensor_tensor(s[0][:], score_ps[0][:], bias0[:], ALU.add)
+        nc.vector.tensor_tensor(part[1][:], bh_win[1][:].indirect(h_list[:]), score1[:], ALU.add)
         val_half = sb([P, T], BF16, "val_half")
-        for j in range(2):
-            nc.scalar.activation(val_half[:, j * T // 2:(j + 1) * T // 2], val_part[j][:], ACT.Copy)
-        gather_vals(0)
-        p = [sb([P, I], F32, "p0", after="val_half"), sb([P, I], F32, "p1", after="val_part1")]
+        nc.scalar.activation(val_half[:], val_win[0][:], ACT.Copy)
+        p = [sb([P, I], F32, "p0", after="val_win0")]
         softmax_head(0)
+        nc.vector.tensor_tensor(s[1][:], bw_win[1][:].indirect(w_list[:]), part[1][:], ALU.add)
+        gather_vals(0)
+        p.append(sb([P, I], F32, "p1", after="val_half"))
         softmax_head(1)
         gather_vals(2)
         inv_sum = sb([P, 2], F32, "inv_sum", after="val_win2")
@@ -171,7 +173,7 @@ def tile_attend_decomposedbias_pl_kernel(tc, query, keys_words, keys_scales, bh,
             v_scales.append(scales[:])
 
         y = sb([P, PACK, Q], F32, "y")
-        out_rows = out_0.rearrange("(p r) q -> r p q", r=PACK)
+        out_rows = out_0.rearrange("(p r) q -> p r q", r=PACK)
         for r, tag in enumerate(("row0", "row1", "o_ps2", "o_ps3")):
             bank = psum.tile([P, Q], F32, name="o_ps%d" % r, tag=tag)
             nc.tensor.matmul_mx(out=bank[:], lhsT=v_codes[r].bitcast(FP8X4), lhsT_scale=v_scales[r],
@@ -180,7 +182,8 @@ def tile_attend_decomposedbias_pl_kernel(tc, query, keys_words, keys_scales, bh,
                 nc.vector.tensor_copy(y[:, r, :], bank[:])
             else:
                 nc.scalar.copy(y[:, r, :], bank[:])
-            nc.sync.dma_start(out_rows[r], y[:, r, :])
+            if r % 2:
+                nc.sync.dma_start(out_rows[:, r - 1:r + 1, :], y[:, r - 1:r + 1, :])
 
         y_grp = sb([P, Q, PACK], BF16, "y_grp")
         nc.vector.tensor_copy(y_grp[:].rearrange("p (c i) t -> p c t i", i=4),

@@ -58,8 +58,8 @@ def tile_attend_decomposedbias_pl_kernel(tc, query, keys_words, keys_scales, bh,
         nc.sync.dma_start(h_list[:], offs2)
         nc.sync.dma_start(bh_win[0][:, :U], bh[0:P, :])
         nc.sync.dma_start(tok_list[:], offs)
-        nc.sync.dma_start(key_words[:].bitcast(I32), keys_words[0].bitcast(I32))
         nc.sync.dma_start(w_list[:], offs3)
+        nc.sync.dma_start(key_words[:].bitcast(I32), keys_words[0].bitcast(I32))
         nc.sync.dma_start(bw_win[0][:, :U], bw[0:P, :])
         nc.sync.dma_start(q_raw[:], query.rearrange("(p j) q -> p j q", j=PACK))
         for g in range(4):
@@ -95,13 +95,13 @@ def tile_attend_decomposedbias_pl_kernel(tc, query, keys_words, keys_scales, bh,
         nc.vector.quantize_mx(out=q_codes[:].bitcast(FP8X4), scales=q_scales[:],
                               in_=q_grp[:].rearrange("p q t -> p (q t)"))
 
-        score_ps = []
-        for h in range(2):
+        score_ps = {}
+        for h in (1, 0):
             bank = psum.tile([P, I], F32, name="score_ps%d" % h, tag="row%d" % h)
             cols = slice(h * P, (h + 1) * P)
             nc.tensor.matmul_mx(out=bank[:], lhsT=q_codes[:, cols].bitcast(FP8X4), lhsT_scale=q_scales[:, cols],
                                 rhs=k_words[:].bitcast(FP4X4), rhs_scale=k_bytes[:], start=True, stop=True)
-            score_ps.append(bank)
+            score_ps[h] = bank
 
         grp_a = sb([P, 4, P, PACK], BF16, "grp_a")
         grp_v = [sb([P, P, PACK], BF16, "grp_v%d" % r) for r in (2, 3)]
@@ -174,6 +174,7 @@ def tile_attend_decomposedbias_pl_kernel(tc, query, keys_words, keys_scales, bh,
 
         y = sb([P, PACK, Q], F32, "y")
         out_rows = out_0.rearrange("(p r) q -> p r q", r=PACK)
+        y_grp = sb([P, Q, PACK], BF16, "y_grp")
         for r, tag in enumerate(("row0", "row1", "o_ps2", "o_ps3")):
             bank = psum.tile([P, Q], F32, name="o_ps%d" % r, tag=tag)
             nc.tensor.matmul_mx(out=bank[:], lhsT=v_codes[r].bitcast(FP8X4), lhsT_scale=v_scales[r],
@@ -183,11 +184,10 @@ def tile_attend_decomposedbias_pl_kernel(tc, query, keys_words, keys_scales, bh,
             else:
                 nc.scalar.copy(y[:, r, :], bank[:])
             if r % 2:
-                nc.sync.dma_start(out_rows[:, r - 1:r + 1, :], y[:, r - 1:r + 1, :])
+                pair = slice(r - 1, r + 1)
+                nc.sync.dma_start(out_rows[:, pair, :], y[:, pair, :])
+                nc.vector.tensor_copy(y_grp[:, :, pair], y[:, pair, :].rearrange("p t q -> p q t"))
 
-        y_grp = sb([P, Q, PACK], BF16, "y_grp")
-        nc.vector.tensor_copy(y_grp[:].rearrange("p (c i) t -> p c t i", i=4),
-                              y[:].rearrange("p t (c i) -> p c t i", i=4))
         y_codes = sb([P, Q], U32, "y_codes")
         y_scales = sb([P, Q], U8, "y_scales")
         nc.vector.quantize_mx(out=y_codes[:].bitcast(FP8X4), scales=y_scales[:],

from contextlib import ExitStack

import concourse.mybir as mybir
from concourse.masks import make_identity

F32 = mybir.dt.float32
BF16 = mybir.dt.bfloat16
I32 = mybir.dt.int32
U32 = mybir.dt.uint32
U16 = mybir.dt.uint16
U8 = mybir.dt.uint8
FP8X4 = mybir.dt.float8_e4m3fn_x4
FP4X4 = mybir.dt.float4_e2m1fn_x4
ALU = mybir.AluOpType
ACT = mybir.ActivationFunctionType
AX = mybir.AxisListType

P = 128
PACK = 4
D, T, I, Q, E, U = 512, 2048, 512, 256, 512, 512
FLOPS = 2 * D * Q * I + 2 * I * E * Q
COPY_WINDOW = 704
ADD_WINDOW = 528


def tile_attend_decomposedbias_pl_kernel(tc, query, keys_words, keys_scales, bh, bw, size, vals,
                                          offs, offs2, offs3, out_0, out_1, out_2):
    nc = tc.nc
    with ExitStack() as ctx:
        keep = ctx.enter_context(tc.tile_pool(name="keep", bufs=1))
        psum = ctx.enter_context(tc.psum_pool(name="psum", bufs=1))

        def sb(shape, dtype, name, after=None):
            return keep.tile(shape, dtype, name=name, tag=after or name, align_bytes=64)

        tok_list = sb([P, I // 16], U16, "tok_list")
        h_list = sb([P, I // 16], U16, "h_list")
        w_list = sb([P, I // 16], U16, "w_list")
        key_words = sb([P, T], U16, "key_words")
        key_bytes = sb([P, T], U8, "key_bytes")
        q_raw = sb([P, PACK, Q], F32, "q_raw")
        bh_win = [sb([P, COPY_WINDOW], F32, "bh_win0"), sb([P, ADD_WINDOW], F32, "bh_win1")]
        bw_win = [sb([P, ADD_WINDOW], F32, "bw_win%d" % h) for h in range(2)]
        val_win = [sb([P, T], F32, "val_win%d" % r) for r in range(PACK)]
        size_col = sb([P, PACK], F32, "size_col")
        ident = sb([P, P], F32, "ident")
        warm = sb([P, 1], F32, "warm")
        warm_out = sb([P, 1], F32, "warm_out")

        nc.vector.memset(key_bytes[:, :T // 2].bitcast(I32), 0)
        nc.gpsimd.memset(key_bytes[:, T // 2:].bitcast(I32), 0)
        for win in bh_win + bw_win:
            nc.vector.memset(win[:, U:], 0.0)
        nc.vector.memset(warm[:], 0.0)
        nc.scalar.activation(warm_out[:], warm[:], ACT.Exp)

        val_rows = vals.rearrange("(p r) t -> r p t", r=PACK)
        nc.sync.dma_start(h_list[:], offs2)
        nc.sync.dma_start(bh_win[0][:, :U], bh[0:P, :])
        nc.sync.dma_start(tok_list[:], offs)
        nc.sync.dma_start(w_list[:], offs3)
        nc.sync.dma_start(key_words[:].bitcast(I32), keys_words[0].bitcast(I32))
        nc.sync.dma_start(bw_win[0][:, :U], bw[0:P, :])
        nc.sync.dma_start(q_raw[:], query.rearrange("(p j) q -> p j q", j=PACK))
        for g in range(4):
            nc.sync.dma_start(key_bytes[32 * g:32 * g + 4, :].bitcast(I32),
                              keys_scales[0, 4 * g:4 * g + 4, :].bitcast(I32))
        nc.sync.dma_start(val_win[1][:], val_rows[1])
        nc.sync.dma_start(bh_win[1][:, :U], bh[P:2 * P, :])
        nc.sync.dma_start(val_win[0][:], val_rows[0])
        nc.sync.dma_start(bw_win[1][:, :U], bw[P:2 * P, :])
        for r in range(2, PACK):
            nc.sync.dma_start(val_win[r][:], val_rows[r])
        nc.gpsimd.dma_start(size_col[:], size.rearrange("o (s t) -> s (o t)", t=PACK))
        make_identity(nc, ident[:])

        size_ps = psum.tile([P, PACK, P], F32, name="size_ps")
        for t in range(PACK):
            nc.tensor.transpose(size_ps[:, t, :], size_col[:, t:t + 1].to_broadcast([P, P]), ident[:])

        part = [sb([P, I], F32, "part%d" % h) for h in range(2)]
        bias0 = sb([P, I], F32, "bias0")
        nc.vector.tensor_copy(part[0][:], bh_win[0][:].indirect(h_list[:]))
        k_words = sb([P, I], U16, "k_words")
        k_bytes = sb([P, I], U8, "k_bytes")
        nc.vector.tensor_copy(k_words[:], key_words[:].indirect(tok_list[:]))
        nc.vector.tensor_tensor(bias0[:], bw_win[0][:].indirect(w_list[:]), part[0][:], ALU.add)
        nc.vector.tensor_copy(k_bytes[:], key_bytes[:].indirect(tok_list[:]))

        q_grp = sb([P, Q, PACK], BF16, "q_grp")
        nc.scalar.copy(q_grp[:].rearrange("p (c i) t -> p c t i", i=4),
                       q_raw[:].rearrange("p t (c i) -> p c t i", i=4))
        q_codes = sb([P, Q], U32, "q_codes")
        q_scales = sb([P, Q], U8, "q_scales")
        nc.vector.quantize_mx(out=q_codes[:].bitcast(FP8X4), scales=q_scales[:],
                              in_=q_grp[:].rearrange("p q t -> p (q t)"))

        score_ps = {}
        for h in (1, 0):
            bank = psum.tile([P, I], F32, name="score_ps%d" % h, tag="row%d" % h)
            cols = slice(h * P, (h + 1) * P)
            nc.tensor.matmul_mx(out=bank[:], lhsT=q_codes[:, cols].bitcast(FP8X4), lhsT_scale=q_scales[:, cols],
                                rhs=k_words[:].bitcast(FP4X4), rhs_scale=k_bytes[:], start=True, stop=True)
            score_ps[h] = bank

        grp_a = sb([P, 4, P, PACK], BF16, "grp_a")
        grp_v = [sb([P, P, PACK], BF16, "grp_v%d" % r) for r in (2, 3)]
        v_dst = [grp_a[:, 2], grp_a[:, 3], grp_v[0][:], grp_v[1][:]]

        def turn(src, dst, bank):
            words = src[:].bitcast(F32)
            for u in range(2):
                nc.tensor.transpose(bank[:, u, :], words[:, u:I // 2:2], ident[:])
            nc.scalar.copy(dst.rearrange("p c t -> p (c t)").bitcast(F32).rearrange("p (c u) -> p c u", u=2),
                           bank[:].rearrange("p u c -> p c u"))

        def gather_vals(r):
            picked = sb([P, I], BF16, "v_picked%d" % r)
            if r == 0:
                nc.scalar.activation(picked[:], val_half[:].indirect(tok_list[:]), ACT.Copy)
            else:
                nc.vector.tensor_copy(picked[:], val_win[r][:].indirect(tok_list[:]))
            bank = psum.tile([P, 2, P], F32, name="v_ps%d" % r, tag="v_ps", bufs=2)
            turn(picked, v_dst[r], bank)

        neg_max = [sb([P, 1], F32, "neg_max%d" % h) for h in range(2)]
        row_sum = sb([P, 2], F32, "row_sum")

        def softmax_head(h):
            nc.vector.tensor_reduce(neg_max[h][:], s[h][:], AX.X, ALU.max, negate=True)
            nc.scalar.activation(p[h][:], s[h][:], ACT.Exp, bias=neg_max[h][:], accum_out=row_sum[:, h:h + 1])

        def weights(h):
            w = sb([P, I], BF16, "w%d" % h)
            nc.vector.scalar_tensor_tensor(w[:].rearrange("p (s t) -> p s t", t=PACK),
                                           p[h][:].rearrange("p (s t) -> p s t", t=PACK), inv_sum[:, h:h + 1],
                                           size_ps[:].rearrange("p t s -> p s t"), ALU.mult, ALU.mult)
            bank = psum.tile([P, 2, P], F32, name="w_ps%d" % h, tag="row%d" % h)
            turn(w, grp_a[:, h], bank)

        score1 = sb([P, I], F32, "score1")
        nc.scalar.copy(score1[:], score_ps[1][:])
        gather_vals(1)
        s = [sb([P, I], F32, "s0", after="val_win1"), sb([P, I], F32, "s1")]
        nc.vector.tensor_tensor(s[0][:], score_ps[0][:], bias0[:], ALU.add)
        nc.vector.tensor_tensor(part[1][:], bh_win[1][:].indirect(h_list[:]), score1[:], ALU.add)
        val_half = sb([P, T], BF16, "val_half")
        nc.scalar.activation(val_half[:], val_win[0][:], ACT.Copy)
        p = [sb([P, I], F32, "p0", after="val_win0")]
        softmax_head(0)
        nc.vector.tensor_tensor(s[1][:], bw_win[1][:].indirect(w_list[:]), part[1][:], ALU.add)
        gather_vals(0)
        p.append(sb([P, I], F32, "p1", after="val_half"))
        softmax_head(1)
        gather_vals(2)
        inv_sum = sb([P, 2], F32, "inv_sum", after="val_win2")
        nc.vector.reciprocal(inv_sum[:], row_sum[:])
        weights(0)
        weights(1)
        gather_vals(3)
        a_codes = sb([P, 4 * P], U32, "a_codes", after="val_win3")
        a_scales = sb([P, 4 * P], U8, "a_scales")
        nc.vector.quantize_mx(out=a_codes[:].bitcast(FP8X4), scales=a_scales[:],
                              in_=grp_a[:].rearrange("p a c t -> p (a c t)"))
        v_codes = [a_codes[:, 2 * P:3 * P], a_codes[:, 3 * P:4 * P]]
        v_scales = [a_scales[:, 2 * P:3 * P], a_scales[:, 3 * P:4 * P]]
        for j in range(2):
            codes = sb([P, P], U32, "b_codes%d" % j)
            scales = sb([P, P], U8, "b_scales%d" % j)
            nc.vector.quantize_mx(out=codes[:].bitcast(FP8X4), scales=scales[:],
                                  in_=grp_v[j][:].rearrange("p c t -> p (c t)"))
            v_codes.append(codes[:])
            v_scales.append(scales[:])

        y = sb([P, PACK, Q], F32, "y")
        out_rows = out_0.rearrange("(p r) q -> p r q", r=PACK)
        y_grp = sb([P, Q, PACK], BF16, "y_grp")
        for r, tag in enumerate(("row0", "row1", "o_ps2", "o_ps3")):
            bank = psum.tile([P, Q], F32, name="o_ps%d" % r, tag=tag)
            nc.tensor.matmul_mx(out=bank[:], lhsT=v_codes[r].bitcast(FP8X4), lhsT_scale=v_scales[r],
                                rhs=a_codes[:, :Q].bitcast(FP8X4), rhs_scale=a_scales[:, :Q], start=True, stop=True)
            if r == 1:
                nc.vector.tensor_copy(y[:, r, :], bank[:])
            else:
                nc.scalar.copy(y[:, r, :], bank[:])
            if r % 2:
                pair = slice(r - 1, r + 1)
                nc.sync.dma_start(out_rows[:, pair, :], y[:, pair, :])
                nc.vector.tensor_copy(y_grp[:, :, pair], y[:, pair, :].rearrange("p t q -> p q t"))

        y_codes = sb([P, Q], U32, "y_codes")
        y_scales = sb([P, Q], U8, "y_scales")
        nc.vector.quantize_mx(out=y_codes[:].bitcast(FP8X4), scales=y_scales[:],
                              in_=y_grp[:].rearrange("p q t -> p (q t)"))
        nc.sync.dma_start(out_1[0].rearrange("p c r -> p (c r)").bitcast(I32), y_codes[:].bitcast(I32))
        for g in range(4):
            queue = nc.scalar if g % 2 else nc.sync
            queue.dma_start(out_2[0, 4 * g:4 * g + 4, :].bitcast(I32), y_scales[32 * g:32 * g + 4, :].bitcast(I32))
